import numpy as np
import ml_dtypes


def mxq(x, axis, fmt="e4m3"):
    dtype, down = {"e4m3": (ml_dtypes.float8_e4m3fn, 7), "e5m2": (ml_dtypes.float8_e5m2, 14)}[fmt]
    v = np.moveaxis(np.asarray(x, np.float32).astype(ml_dtypes.bfloat16).astype(np.float64), axis, -1)
    blocks = v.reshape(v.shape[:-1] + (-1, 32))
    amax = np.abs(blocks).max(-1, keepdims=True)
    byte = np.maximum(np.where(amax > 0, np.frexp(amax)[1] - 1 + 127, 0) - down, 1)
    scale = np.exp2(byte - 127.0)
    codes = (blocks / scale).astype(np.float32).astype(dtype).astype(np.float64)
    return np.moveaxis((codes * scale).reshape(v.shape), -1, axis)


WIDE = False


def mx_kscale(k):
    if not WIDE:
        return np.ones(k)
    levels = np.array([30, -30])
    if k % 512:
        return np.exp2(np.random.permutation(np.resize(levels, k // 32))).repeat(32)
    a = np.empty((k // 512, 16))
    for p in range(k // 512):
        a[p, :8] = np.random.permutation(np.resize(levels, 8))
        for g in range(8):
            far = levels[np.abs(levels - a[p, g]) >= 10]
            a[p, g + 8] = far[np.random.randint(len(far))]
    return np.exp2(a.ravel()).repeat(32)


def f64(x):
    return np.asarray(x).astype(np.float64)


def striped(idx):
    return np.tile(np.asarray(idx).reshape(-1, 16).T, (8, 1)).astype(np.uint16)


def unstriped(offs):
    return offs[:16].T.reshape(-1).astype(np.int64)


E2M1 = np.array([0.0, 0.5, 1.0, 1.5, 2.0, 3.0, 4.0, 6.0, -0.0, -0.5, -1.0, -1.5, -2.0, -3.0, -4.0, -6.0])


def pack_weight(w, fmt):
    k, n = w.shape
    w = f64(np.asarray(w, np.float32).astype(ml_dtypes.bfloat16)).reshape(k // 32, 32, n)
    amax = np.abs(w).max(1)
    if fmt in ("e4m3", "e5m2"):
        byte = np.frexp(amax)[1] - 1 + 127 - (7 if fmt == "e4m3" else 14)
    else:
        mant, ex = np.frexp(amax / 6.0)
        byte = np.where(mant > 0.5, ex, ex - 1) + 127
    byte = np.clip(np.where(amax > 0, byte, 1), 1, 254)
    scaled = (w * np.exp2(127.0 - byte)[:, None, :]).reshape(k, n).astype(np.float32)
    by_word = np.ascontiguousarray(scaled.reshape(k // 512, 128, 4, n).transpose(0, 1, 3, 2))
    if fmt in ("e4m3", "e5m2"):
        words = by_word.astype(ml_dtypes.float8_e4m3fn if fmt == "e4m3" else ml_dtypes.float8_e5m2).view(np.uint8)
    else:
        c = by_word.astype(ml_dtypes.float4_e2m1fn).view(np.uint8) & 0xF
        words = (c[..., 0::2] | (c[..., 1::2] << 4)).reshape(k // 512, 128, 2 * n)
    return np.ascontiguousarray(words), np.ascontiguousarray(byte.astype(np.uint8).reshape(k // 512, 16, n))


def unpack_weight(words, scales, fmt):
    g, _, n = scales.shape
    words = np.ascontiguousarray(words).reshape(g, 128, n, -1)
    if fmt in ("e4m3", "e5m2"):
        vals = words.view(ml_dtypes.float8_e4m3fn if fmt == "e4m3" else ml_dtypes.float8_e5m2).astype(np.float64)
    else:
        nib = np.empty((g, 128, n, 4), np.uint8)
        nib[..., 0::2] = words & 0xF
        nib[..., 1::2] = words >> 4
        vals = E2M1[nib]
    vals = vals * np.repeat(np.exp2(scales.astype(np.float64) - 127.0), 8, axis=1)[..., None]
    return vals.transpose(0, 1, 3, 2).reshape(g * 512, n)


K, T, Z, J, R, N, E = 512, 1024, 1024, 256, 512, 256, 1024


def setup_inputs():
    n = np.random.standard_normal
    idx = np.random.permutation(T)[:J]
    idx2 = np.random.permutation(Z)[:J]
    idx3 = np.random.permutation(E)[:J]
    fk = mx_kscale(K)
    fr = mx_kscale(R)
    xtp = pack_weight(n((K, T)) / fk[:, None], "e4m3")
    xop = pack_weight(n((K, Z)) / fk[:, None], "e2m1")
    wp = pack_weight(n((K, R)) * 1 / np.sqrt(K) * fk[:, None] * fr, "e5m2")
    w2p = pack_weight(n((K, R)) * 1 / np.sqrt(K) * fk[:, None] * fr, "e5m2")
    wbp = pack_weight(n((R, N)) * 1 / np.sqrt(R) / fr[:, None], "e5m2")
    return {
        "xt_words": xtp[0],
        "xt_scales": xtp[1],
        "xo_words": xop[0],
        "xo_scales": xop[1],
        "w_words": wp[0],
        "w_scales": wp[1],
        "w2_words": w2p[0],
        "w2_scales": w2p[1],
        "wb_words": wbp[0],
        "wb_scales": wbp[1],
        "offs": striped(idx),
        "offs2": striped(idx2),
        "offs3": striped(idx3),
    }


def reference(xt_words, xt_scales, xo_words, xo_scales, w_words, w_scales, w2_words, w2_scales, wb_words, wb_scales, offs, offs2, offs3):
    idx = unstriped(offs)
    idx2 = unstriped(offs2)
    idx3 = unstriped(offs3)
    xtu = unpack_weight(xt_words, xt_scales, "e4m3")
    xou = unpack_weight(xo_words, xo_scales, "e2m1")
    wu = unpack_weight(w_words, w_scales, "e5m2")
    w2u = unpack_weight(w2_words, w2_scales, "e5m2")
    wbu = unpack_weight(wb_words, wb_scales, "e5m2")
    xtidxg = xtu[:, idx]
    xoidx2g = xou[:, idx2]
    a = wu.T @ xtidxg + w2u.T @ xoidx2g
    b = w2u.T @ xtidxg + wu.T @ xoidx2g
    hid = np.abs(a - b)
    hidq = mxq(hid, 0, "e4m3")
    p = wbu.T @ hidq
    y = np.zeros((N, E))
    y[:, idx3] = p
    return y

@@ -1,0 +1,166 @@
+import concourse.mybir as mybir
+
+F32 = mybir.dt.float32
+BF16 = mybir.dt.bfloat16
+I32 = mybir.dt.int32
+U32 = mybir.dt.uint32
+U16 = mybir.dt.uint16
+U8 = mybir.dt.uint8
+E4M3 = mybir.dt.float8_e4m3fn_x4
+E5M2 = mybir.dt.float8_e5m2_x4
+E2M1 = mybir.dt.float4_e2m1fn_x4
+ACT = mybir.ActivationFunctionType
+ALU = mybir.AluOpType
+
+P = 128
+K, T, Z, J, R, N, E = 512, 1024, 1024, 256, 512, 256, 1024
+PACK = 4
+HALF = 128
+HALVES = J // HALF
+COLS = HALF // 16
+
+FLOPS = 2 * (4 * K * R * J + R * N * J)
+
+
+def tile_list_crossed_direct_one_scattered_kernel(
+    tc, xt_words, xt_scales, xo_words, xo_scales, w_words, w_scales, w2_words, w2_scales,
+    wb_words, wb_scales, offs, offs2, offs3, out
+):
+    nc = tc.nc
+    with tc.tile_pool(name="sb", bufs=1) as sb, tc.psum_pool(name="ps", bufs=1) as ps:
+
+        def tile(name, shape, dtype):
+            return sb.tile(shape, dtype, name=name, align_bytes=64)
+
+        def words_of(ap):
+            return ap[0].rearrange("p n t -> p (n t)").bitcast(I32)
+
+        def load_live_rows(engine, plane, scales):
+            for q in range(4):
+                engine.dma_start(
+                    plane[32 * q : 32 * q + 4, :].bitcast(I32), scales[0, 4 * q : 4 * q + 4, :].bitcast(I32)
+                )
+
+        xt_list = tile("xt_list", [P, J // 16], U16)
+        xo_list = tile("xo_list", [P, J // 16], U16)
+        out_list = tile("out_list", [P, J // 16], U16)
+        xt_table = tile("xt_table", [P, T], U32)
+        xo_table = tile("xo_table", [P, Z], U16)
+        xt_plane = tile("xt_plane", [P, T], U8)
+        xo_plane = tile("xo_plane", [P, Z], U8)
+        w_raw = [tile("w_raw%d" % i, [P, R], U32) for i in range(2)]
+        w_plane_raw = [tile("w_plane_raw%d" % i, [P, R], U8) for i in range(2)]
+        w_codes = [tile("w_codes%d" % i, [P, PACK, P], U32) for i in range(2)]
+        w_plane = [tile("w_plane%d" % i, [P, PACK, P], U8) for i in range(2)]
+        wb_codes = tile("wb_codes", [P, N], U32)
+        wb_plane = tile("wb_plane", [P, N], U8)
+        pages = [tile("page%d" % i, [P, E], F32) for i in range(N // P)]
+
+        for plane in (w_plane_raw[0], xo_plane, xt_plane, w_plane_raw[1], wb_plane):
+            nc.vector.memset(plane[:].bitcast(I32), 0)
+
+        nc.sync.dma_start(xt_list[:], offs)
+        nc.sync.dma_start(xo_list[:], offs2)
+        nc.sync.dma_start(w_raw[0][:].bitcast(I32), words_of(w_words))
+        load_live_rows(nc.sync, w_plane_raw[0], w_scales)
+        nc.sync.dma_start(xt_table[:].bitcast(I32), words_of(xt_words))
+        load_live_rows(nc.gpsimd, xo_plane, xo_scales)
+        load_live_rows(nc.sync, xt_plane, xt_scales)
+        nc.sync.dma_start(w_raw[1][:].bitcast(I32), words_of(w2_words))
+        nc.sync.dma_start(xo_table[:].bitcast(I32), xo_words[0].bitcast(I32))
+        load_live_rows(nc.sync, w_plane_raw[1], w2_scales)
+        nc.sync.dma_start(wb_codes[:].bitcast(I32), words_of(wb_words))
+        load_live_rows(nc.sync, wb_plane, wb_scales)
+        nc.sync.dma_start(out_list[:], offs3)
+
+        for page in pages:
+            nc.vector.memset(page[:], 0.0)
+
+        def deal(i):
+            nc.scalar.copy(
+                w_codes[i][:].rearrange("p t (c i) -> p c t i", i=4),
+                w_raw[i][:].rearrange("p (c i t) -> p c t i", i=4, t=PACK),
+            )
+            nc.vector.tensor_copy(
+                w_plane[i][:].rearrange("p t (c i) -> p c t i", i=16),
+                w_plane_raw[i][:].rearrange("p (c i t) -> p c t i", i=16, t=PACK),
+            )
+
+        def pick(name, h, table, plane, offsets, dtype):
+            codes = tile("%s_codes%d" % (name, h), [P, HALF], dtype)
+            scales = tile("%s_scales%d" % (name, h), [P, HALF], U8)
+            part = offsets[:, h * COLS : (h + 1) * COLS]
+            nc.vector.tensor_copy(codes[:], table[:].indirect(part))
+            nc.vector.tensor_copy(scales[:], plane[:].indirect(part))
+            return codes, scales
+
+        deal(0)
+        xt = [pick("xt", h, xt_table, xt_plane, xt_list, U32) for h in range(HALVES)]
+        deal(1)
+        xo = [pick("xo", h, xo_table, xo_plane, xo_list, U16) for h in range(HALVES)]
+
+        def passes(acc, i, picked, fmt):
+            codes, scales = picked
+            for t in range(PACK):
+                nc.tensor.matmul_mx(
+                    acc[:, t, :],
+                    lhsT=w_codes[i][:, t, :].bitcast(E5M2),
+                    lhsT_scale=w_plane[i][:, t, :],
+                    rhs=codes[:].bitcast(fmt),
+                    rhs_scale=scales[:],
+                    start=(fmt is E4M3 and t == 0),
+                    stop=(fmt is E2M1 and t == PACK - 1),
+                )
+
+        a_ps = [ps.tile([P, PACK, HALF], F32, name="a%d" % h) for h in range(HALVES)]
+        b_ps = [ps.tile([P, PACK, HALF], F32, name="b%d" % h) for h in range(HALVES)]
+        for h in range(HALVES):
+            passes(a_ps[h], 0, xt[h], E4M3)
+        for h in range(HALVES):
+            passes(b_ps[h], 1, xt[h], E4M3)
+
+        a_sb = []
+        for h in range(HALVES):
+            passes(a_ps[h], 1, xo[h], E2M1)
+            a_sb.append(tile("a_sb%d" % h, [P, HALF, PACK], F32))
+            nc.scalar.activation(a_sb[h][:], a_ps[h][:].rearrange("p t j -> p j t"), ACT.Copy)
+
+        hid = []
+        for h in range(HALVES):
+            passes(b_ps[h], 0, xo[h], E2M1)
+            diff = tile("diff%d" % h, [P, HALF, PACK], F32)
+            nc.vector.tensor_tensor(diff[:], b_ps[h][:].rearrange("p t j -> p j t"), a_sb[h][:], ALU.subtract)
+            hid.append(tile("hid%d" % h, [P, HALF * PACK], BF16))
+            nc.scalar.activation(hid[h][:], diff[:].rearrange("p j t -> p (j t)"), ACT.Abs)
+
+        p_ps = []
+        for h in range(HALVES):
+            codes = tile("hid_codes%d" % h, [P, HALF], U32)
+            scales = tile("hid_scales%d" % h, [P, HALF], U8)
+            nc.vector.quantize_mx(codes[:].bitcast(E4M3), scales[:], hid[h][:])
+            banks = []
+            for n in range(N // P):
+                acc = ps.tile([P, HALF], F32, name="p%d_%d" % (h, n))
+                nc.tensor.matmul_mx(
+                    acc[:],
+                    lhsT=wb_codes[:, n * P : (n + 1) * P].bitcast(E5M2),
+                    lhsT_scale=wb_plane[:, n * P : (n + 1) * P],
+                    rhs=codes[:].bitcast(E4M3),
+                    rhs_scale=scales[:],
+                    start=True,
+                    stop=True,
+                )
+                banks.append(acc)
+            p_ps.append(banks)
+
+        for h in range(HALVES):
+            part = out_list[:, h * COLS : (h + 1) * COLS]
+            low = tile("p_low%d" % h, [P, HALF], F32)
+            nc.vector.tensor_copy(low[:], p_ps[h][0][:])
+            nc.vector.tensor_copy(pages[0][:].indirect(part), low[:])
+            high = tile("p_high%d" % h, [P, HALF], F32)
+            nc.scalar.activation(high[:], p_ps[h][1][:], ACT.Copy)
+            nc.scalar.activation(pages[1][:].indirect(part), high[:], ACT.Copy)
+
+        nc.sync.dma_start(out[0:P, :], pages[0][:])
+        nc.scalar.dma_start(out[P : 2 * P, :], pages[1][:])

@@ -35,9 +35,9 @@ def tile_list_crossed_direct_one_scattered_kernel(
         def words_of(ap):
             return ap[0].rearrange("p n t -> p (n t)").bitcast(I32)
 
-        def load_live_rows(engine, plane, scales):
-            for q in range(4):
-                engine.dma_start(
+        def load_live_rows(plane, scales, quadrants=range(4)):
+            for q in quadrants:
+                nc.sync.dma_start(
                     plane[32 * q : 32 * q + 4, :].bitcast(I32), scales[0, 4 * q : 4 * q + 4, :].bitcast(I32)
                 )
 
@@ -56,22 +56,23 @@ def tile_list_crossed_direct_one_scattered_kernel(
         wb_plane = tile("wb_plane", [P, N], U8)
         pages = [tile("page%d" % i, [P, E], F32) for i in range(N // P)]
 
-        for plane in (w_plane_raw[0], xo_plane, xt_plane, w_plane_raw[1], wb_plane):
+        for plane in (w_plane_raw[0], xt_plane, w_plane_raw[1], xo_plane, wb_plane):
             nc.vector.memset(plane[:].bitcast(I32), 0)
 
         nc.sync.dma_start(xt_list[:], offs)
         nc.sync.dma_start(xo_list[:], offs2)
         nc.sync.dma_start(w_raw[0][:].bitcast(I32), words_of(w_words))
-        load_live_rows(nc.sync, w_plane_raw[0], w_scales)
+        load_live_rows(w_plane_raw[0], w_scales)
         nc.sync.dma_start(xt_table[:].bitcast(I32), words_of(xt_words))
-        load_live_rows(nc.gpsimd, xo_plane, xo_scales)
-        load_live_rows(nc.sync, xt_plane, xt_scales)
+        load_live_rows(xt_plane, xt_scales)
+        load_live_rows(w_plane_raw[1], w2_scales, range(0, 2))
         nc.sync.dma_start(w_raw[1][:].bitcast(I32), words_of(w2_words))
         nc.sync.dma_start(xo_table[:].bitcast(I32), xo_words[0].bitcast(I32))
-        load_live_rows(nc.sync, w_plane_raw[1], w2_scales)
+        load_live_rows(w_plane_raw[1], w2_scales, range(2, 4))
+        load_live_rows(xo_plane, xo_scales)
         nc.sync.dma_start(wb_codes[:].bitcast(I32), words_of(wb_words))
-        load_live_rows(nc.sync, wb_plane, wb_scales)
         nc.sync.dma_start(out_list[:], offs3)
+        load_live_rows(wb_plane, wb_scales)
 
         for page in pages:
             nc.vector.memset(page[:], 0.0)
@@ -119,27 +120,26 @@ def tile_list_crossed_direct_one_scattered_kernel(
         for h in range(HALVES):
             passes(b_ps[h], 1, xt[h], E4M3)
 
-        a_sb = []
-        for h in range(HALVES):
-            passes(a_ps[h], 1, xo[h], E2M1)
-            a_sb.append(tile("a_sb%d" % h, [P, HALF, PACK], F32))
-            nc.scalar.activation(a_sb[h][:], a_ps[h][:].rearrange("p t j -> p j t"), ACT.Copy)
-
         hid = []
         for h in range(HALVES):
+            passes(a_ps[h], 1, xo[h], E2M1)
+            a_sb = tile("a_sb%d" % h, [P, HALF, PACK], F32)
+            nc.scalar.activation(a_sb[:], a_ps[h][:].rearrange("p t j -> p j t"), ACT.Copy)
             passes(b_ps[h], 0, xo[h], E2M1)
             diff = tile("diff%d" % h, [P, HALF, PACK], F32)
-            nc.vector.tensor_tensor(diff[:], b_ps[h][:].rearrange("p t j -> p j t"), a_sb[h][:], ALU.subtract)
-            hid.append(tile("hid%d" % h, [P, HALF * PACK], BF16))
-            nc.scalar.activation(hid[h][:], diff[:].rearrange("p j t -> p (j t)"), ACT.Abs)
+            nc.vector.tensor_tensor(diff[:], b_ps[h][:].rearrange("p t j -> p j t"), a_sb[:], ALU.subtract)
+            hid.append((tile("hid%d" % h, [P, HALF * PACK], BF16), diff))
+        for h in range(HALVES):
+            nc.scalar.activation(hid[h][0][:], hid[h][1][:].rearrange("p j t -> p (j t)"), ACT.Abs)
 
-        p_ps = []
+        p_high = tile("p_high", [P, J], F32)
+        p_low = []
         for h in range(HALVES):
             codes = tile("hid_codes%d" % h, [P, HALF], U32)
             scales = tile("hid_scales%d" % h, [P, HALF], U8)
-            nc.vector.quantize_mx(codes[:].bitcast(E4M3), scales[:], hid[h][:])
-            banks = []
-            for n in range(N // P):
+            nc.vector.quantize_mx(codes[:].bitcast(E4M3), scales[:], hid[h][0][:])
+            p_low.append(tile("p_low%d" % h, [P, HALF], F32))
+            for n, p_sb in enumerate((p_low[h][:], p_high[:, h * HALF : (h + 1) * HALF])):
                 acc = ps.tile([P, HALF], F32, name="p%d_%d" % (h, n))
                 nc.tensor.matmul_mx(
                     acc[:],
@@ -150,17 +150,11 @@ def tile_list_crossed_direct_one_scattered_kernel(
                     start=True,
                     stop=True,
                 )
-                banks.append(acc)
-            p_ps.append(banks)
+                nc.scalar.activation(p_sb, acc[:], ACT.Copy)
 
         for h in range(HALVES):
-            part = out_list[:, h * COLS : (h + 1) * COLS]
-            low = tile("p_low%d" % h, [P, HALF], F32)
-            nc.vector.tensor_copy(low[:], p_ps[h][0][:])
-            nc.vector.tensor_copy(pages[0][:].indirect(part), low[:])
-            high = tile("p_high%d" % h, [P, HALF], F32)
-            nc.scalar.activation(high[:], p_ps[h][1][:], ACT.Copy)
-            nc.scalar.activation(pages[1][:].indirect(part), high[:], ACT.Copy)
+            nc.vector.tensor_copy(pages[0][:].indirect(out_list[:, h * COLS : (h + 1) * COLS]), p_low[h][:])
+        nc.scalar.activation(pages[1][:].indirect(out_list[:]), p_high[:], ACT.Copy)
 
-        nc.sync.dma_start(out[0:P, :], pages[0][:])
-        nc.scalar.dma_start(out[P : 2 * P, :], pages[1][:])
+        for n, page in enumerate(pages):
+            nc.sync.dma_start(out[n * P : (n + 1) * P, :], page[:])

@@ -100,7 +100,7 @@ def tile_list_crossed_direct_one_scattered_kernel(
         deal(1)
         xo = [pick("xo", h, xo_table, xo_plane, xo_list, U16) for h in range(HALVES)]
 
-        def passes(acc, i, picked, fmt):
+        def passes(acc, i, picked, fmt, first):
             codes, scales = picked
             for t in range(PACK):
                 nc.tensor.matmul_mx(
@@ -109,28 +109,38 @@ def tile_list_crossed_direct_one_scattered_kernel(
                     lhsT_scale=w_plane[i][:, t, :],
                     rhs=codes[:].bitcast(fmt),
                     rhs_scale=scales[:],
-                    start=(fmt is E4M3 and t == 0),
-                    stop=(fmt is E2M1 and t == PACK - 1),
+                    start=(first and t == 0),
+                    stop=(not first and t == PACK - 1),
                 )
 
         a_ps = [ps.tile([P, PACK, HALF], F32, name="a%d" % h) for h in range(HALVES)]
         b_ps = [ps.tile([P, PACK, HALF], F32, name="b%d" % h) for h in range(HALVES)]
         for h in range(HALVES):
-            passes(a_ps[h], 0, xt[h], E4M3)
-        for h in range(HALVES):
-            passes(b_ps[h], 1, xt[h], E4M3)
+            passes(a_ps[h], 0, xt[h], E4M3, True)
 
+        PIECE = HALF // 2
         hid = []
+        diffs = []
         for h in range(HALVES):
-            passes(a_ps[h], 1, xo[h], E2M1)
-            a_sb = tile("a_sb%d" % h, [P, HALF, PACK], F32)
-            nc.scalar.activation(a_sb[:], a_ps[h][:].rearrange("p t j -> p j t"), ACT.Copy)
-            passes(b_ps[h], 0, xo[h], E2M1)
-            diff = tile("diff%d" % h, [P, HALF, PACK], F32)
-            nc.vector.tensor_tensor(diff[:], b_ps[h][:].rearrange("p t j -> p j t"), a_sb[:], ALU.subtract)
-            hid.append((tile("hid%d" % h, [P, HALF * PACK], BF16), diff))
-        for h in range(HALVES):
-            nc.scalar.activation(hid[h][0][:], hid[h][1][:].rearrange("p j t -> p (j t)"), ACT.Abs)
+            if h == 0:
+                passes(b_ps[h], 1, xt[h], E4M3, True)
+            passes(a_ps[h], 1, xo[h], E2M1, False)
+            a_sb = []
+            for j in range(0, HALF, PIECE):
+                a_sb.append(tile("a_sb%d_%d" % (h, j), [P, PIECE, PACK], F32))
+                nc.scalar.activation(a_sb[-1][:], a_ps[h][:, :, j : j + PIECE].rearrange("p t j -> p j t"), ACT.Copy)
+            passes(b_ps[h], 0, xo[h], E2M1, h == 1)
+            if h == 1:
+                passes(b_ps[h], 1, xt[h], E4M3, False)
+            hid.append((tile("hid%d" % h, [P, HALF * PACK], BF16), None))
+            for u, j in enumerate(range(0, HALF, PIECE)):
+                diff = tile("diff%d_%d" % (h, j), [P, PIECE, PACK], F32)
+                nc.vector.tensor_tensor(
+                    diff[:], b_ps[h][:, :, j : j + PIECE].rearrange("p t j -> p j t"), a_sb[u][:], ALU.subtract
+                )
+                nc.scalar.activation(
+                    hid[h][0][:, j * PACK : (j + PIECE) * PACK], diff[:].rearrange("p j t -> p (j t)"), ACT.Abs
+                )
 
         p_high = tile("p_high", [P, J], F32)
         p_low = []

@@ -35,9 +35,9 @@ def tile_list_crossed_direct_one_scattered_kernel(
         def words_of(ap):
             return ap[0].rearrange("p n t -> p (n t)").bitcast(I32)
 
-        def load_live_rows(plane, scales, quadrants=range(4)):
+        def load_live_rows(plane, scales, quadrants=range(4), queue=nc.sync):
             for q in quadrants:
-                nc.sync.dma_start(
+                queue.dma_start(
                     plane[32 * q : 32 * q + 4, :].bitcast(I32), scales[0, 4 * q : 4 * q + 4, :].bitcast(I32)
                 )
 
@@ -56,9 +56,10 @@ def tile_list_crossed_direct_one_scattered_kernel(
         wb_plane = tile("wb_plane", [P, N], U8)
         pages = [tile("page%d" % i, [P, E], F32) for i in range(N // P)]
 
-        for plane in (w_plane_raw[0], xt_plane, w_plane_raw[1], xo_plane, wb_plane):
+        for plane in (w_plane_raw[0], w_plane_raw[1], xt_plane, xo_plane, wb_plane):
             nc.vector.memset(plane[:].bitcast(I32), 0)
 
+        load_live_rows(w_plane_raw[1], w2_scales, range(2, 4), nc.gpsimd)
         nc.sync.dma_start(xt_list[:], offs)
         nc.sync.dma_start(xo_list[:], offs2)
         nc.sync.dma_start(w_raw[0][:].bitcast(I32), words_of(w_words))
@@ -68,7 +69,7 @@ def tile_list_crossed_direct_one_scattered_kernel(
         load_live_rows(w_plane_raw[1], w2_scales, range(0, 2))
         nc.sync.dma_start(w_raw[1][:].bitcast(I32), words_of(w2_words))
         nc.sync.dma_start(xo_table[:].bitcast(I32), xo_words[0].bitcast(I32))
-        load_live_rows(w_plane_raw[1], w2_scales, range(2, 4))
+
         load_live_rows(xo_plane, xo_scales)
         nc.sync.dma_start(wb_codes[:].bitcast(I32), words_of(wb_words))
         nc.sync.dma_start(out_list[:], offs3)

import concourse.mybir as mybir

F32 = mybir.dt.float32
BF16 = mybir.dt.bfloat16
I32 = mybir.dt.int32
U32 = mybir.dt.uint32
U16 = mybir.dt.uint16
U8 = mybir.dt.uint8
E4M3 = mybir.dt.float8_e4m3fn_x4
E5M2 = mybir.dt.float8_e5m2_x4
E2M1 = mybir.dt.float4_e2m1fn_x4
ACT = mybir.ActivationFunctionType
ALU = mybir.AluOpType

P = 128
K, T, Z, J, R, N, E = 512, 1024, 1024, 256, 512, 256, 1024
PACK = 4
HALF = 128
HALVES = J // HALF
COLS = HALF // 16

FLOPS = 2 * (4 * K * R * J + R * N * J)


def tile_list_crossed_direct_one_scattered_kernel(
    tc, xt_words, xt_scales, xo_words, xo_scales, w_words, w_scales, w2_words, w2_scales,
    wb_words, wb_scales, offs, offs2, offs3, out
):
    nc = tc.nc
    with tc.tile_pool(name="sb", bufs=1) as sb, tc.psum_pool(name="ps", bufs=1) as ps:

        def tile(name, shape, dtype):
            return sb.tile(shape, dtype, name=name, align_bytes=64)

        def words_of(ap):
            return ap[0].rearrange("p n t -> p (n t)").bitcast(I32)

        def load_live_rows(plane, scales, quadrants=range(4), queue=nc.sync):
            for q in quadrants:
                queue.dma_start(
                    plane[32 * q : 32 * q + 4, :].bitcast(I32), scales[0, 4 * q : 4 * q + 4, :].bitcast(I32)
                )

        xt_list = tile("xt_list", [P, J // 16], U16)
        xo_list = tile("xo_list", [P, J // 16], U16)
        out_list = tile("out_list", [P, J // 16], U16)
        xt_table = tile("xt_table", [P, T], U32)
        xo_table = tile("xo_table", [P, Z], U16)
        xt_plane = tile("xt_plane", [P, T], U8)
        xo_plane = tile("xo_plane", [P, Z], U8)
        w_raw = [tile("w_raw%d" % i, [P, R], U32) for i in range(2)]
        w_plane_raw = [tile("w_plane_raw%d" % i, [P, R], U8) for i in range(2)]
        w_codes = [tile("w_codes%d" % i, [P, PACK, P], U32) for i in range(2)]
        w_plane = [tile("w_plane%d" % i, [P, PACK, P], U8) for i in range(2)]
        wb_codes = tile("wb_codes", [P, N], U32)
        wb_plane = tile("wb_plane", [P, N], U8)
        pages = [tile("page%d" % i, [P, E], F32) for i in range(N // P)]

        for plane in (w_plane_raw[0], w_plane_raw[1], xt_plane, xo_plane, wb_plane):
            nc.vector.memset(plane[:].bitcast(I32), 0)

        load_live_rows(w_plane_raw[1], w2_scales, range(2, 4), nc.gpsimd)
        nc.sync.dma_start(xt_list[:], offs)
        nc.sync.dma_start(xo_list[:], offs2)
        nc.sync.dma_start(w_raw[0][:].bitcast(I32), words_of(w_words))
        load_live_rows(w_plane_raw[0], w_scales)
        nc.sync.dma_start(xt_table[:].bitcast(I32), words_of(xt_words))
        load_live_rows(xt_plane, xt_scales)
        load_live_rows(w_plane_raw[1], w2_scales, range(0, 2))
        nc.sync.dma_start(w_raw[1][:].bitcast(I32), words_of(w2_words))
        nc.sync.dma_start(xo_table[:].bitcast(I32), xo_words[0].bitcast(I32))

        load_live_rows(xo_plane, xo_scales)
        nc.sync.dma_start(wb_codes[:].bitcast(I32), words_of(wb_words))
        nc.sync.dma_start(out_list[:], offs3)
        load_live_rows(wb_plane, wb_scales)

        for page in pages:
            nc.vector.memset(page[:], 0.0)

        def deal(i):
            nc.scalar.copy(
                w_codes[i][:].rearrange("p t (c i) -> p c t i", i=4),
                w_raw[i][:].rearrange("p (c i t) -> p c t i", i=4, t=PACK),
            )
            nc.vector.tensor_copy(
                w_plane[i][:].rearrange("p t (c i) -> p c t i", i=16),
                w_plane_raw[i][:].rearrange("p (c i t) -> p c t i", i=16, t=PACK),
            )

        def pick(name, h, table, plane, offsets, dtype):
            codes = tile("%s_codes%d" % (name, h), [P, HALF], dtype)
            scales = tile("%s_scales%d" % (name, h), [P, HALF], U8)
            part = offsets[:, h * COLS : (h + 1) * COLS]
            nc.vector.tensor_copy(codes[:], table[:].indirect(part))
            nc.vector.tensor_copy(scales[:], plane[:].indirect(part))
            return codes, scales

        deal(0)
        xt = [pick("xt", h, xt_table, xt_plane, xt_list, U32) for h in range(HALVES)]
        deal(1)
        xo = [pick("xo", h, xo_table, xo_plane, xo_list, U16) for h in range(HALVES)]

        def passes(acc, i, picked, fmt, first):
            codes, scales = picked
            for t in range(PACK):
                nc.tensor.matmul_mx(
                    acc[:, t, :],
                    lhsT=w_codes[i][:, t, :].bitcast(E5M2),
                    lhsT_scale=w_plane[i][:, t, :],
                    rhs=codes[:].bitcast(fmt),
                    rhs_scale=scales[:],
                    start=(first and t == 0),
                    stop=(not first and t == PACK - 1),
                )

        a_ps = [ps.tile([P, PACK, HALF], F32, name="a%d" % h) for h in range(HALVES)]
        b_ps = [ps.tile([P, PACK, HALF], F32, name="b%d" % h) for h in range(HALVES)]
        for h in range(HALVES):
            passes(a_ps[h], 0, xt[h], E4M3, True)

        PIECE = HALF // 2
        hid = []
        diffs = []
        for h in range(HALVES):
            if h == 0:
                passes(b_ps[h], 1, xt[h], E4M3, True)
            passes(a_ps[h], 1, xo[h], E2M1, False)
            a_sb = []
            for j in range(0, HALF, PIECE):
                a_sb.append(tile("a_sb%d_%d" % (h, j), [P, PIECE, PACK], F32))
                nc.scalar.activation(a_sb[-1][:], a_ps[h][:, :, j : j + PIECE].rearrange("p t j -> p j t"), ACT.Copy)
            passes(b_ps[h], 0, xo[h], E2M1, h == 1)
            if h == 1:
                passes(b_ps[h], 1, xt[h], E4M3, False)
            hid.append((tile("hid%d" % h, [P, HALF * PACK], BF16), None))
            for u, j in enumerate(range(0, HALF, PIECE)):
                diff = tile("diff%d_%d" % (h, j), [P, PIECE, PACK], F32)
                nc.vector.tensor_tensor(
                    diff[:], b_ps[h][:, :, j : j + PIECE].rearrange("p t j -> p j t"), a_sb[u][:], ALU.subtract
                )
                nc.scalar.activation(
                    hid[h][0][:, j * PACK : (j + PIECE) * PACK], diff[:].rearrange("p j t -> p (j t)"), ACT.Abs
                )

        p_high = tile("p_high", [P, J], F32)
        p_low = []
        for h in range(HALVES):
            codes = tile("hid_codes%d" % h, [P, HALF], U32)
            scales = tile("hid_scales%d" % h, [P, HALF], U8)
            nc.vector.quantize_mx(codes[:].bitcast(E4M3), scales[:], hid[h][0][:])
            p_low.append(tile("p_low%d" % h, [P, HALF], F32))
            for n, p_sb in enumerate((p_low[h][:], p_high[:, h * HALF : (h + 1) * HALF])):
                acc = ps.tile([P, HALF], F32, name="p%d_%d" % (h, n))
                nc.tensor.matmul_mx(
                    acc[:],
                    lhsT=wb_codes[:, n * P : (n + 1) * P].bitcast(E5M2),
                    lhsT_scale=wb_plane[:, n * P : (n + 1) * P],
                    rhs=codes[:].bitcast(E4M3),
                    rhs_scale=scales[:],
                    start=True,
                    stop=True,
                )
                nc.scalar.activation(p_sb, acc[:], ACT.Copy)

        for h in range(HALVES):
            nc.vector.tensor_copy(pages[0][:].indirect(out_list[:, h * COLS : (h + 1) * COLS]), p_low[h][:])
        nc.scalar.activation(pages[1][:].indirect(out_list[:]), p_high[:], ACT.Copy)

        for n, page in enumerate(pages):
            nc.sync.dma_start(out[n * P : (n + 1) * P, :], page[:])
